import numpy as np
import ml_dtypes


def mxq(x, axis, fmt="e4m3"):
    dtype, down = {"e4m3": (ml_dtypes.float8_e4m3fn, 7), "e5m2": (ml_dtypes.float8_e5m2, 14)}[fmt]
    v = np.moveaxis(np.asarray(x, np.float32).astype(ml_dtypes.bfloat16).astype(np.float64), axis, -1)
    blocks = v.reshape(v.shape[:-1] + (-1, 32))
    amax = np.abs(blocks).max(-1, keepdims=True)
    byte = np.maximum(np.where(amax > 0, np.frexp(amax)[1] - 1 + 127, 0) - down, 1)
    scale = np.exp2(byte - 127.0)
    codes = (blocks / scale).astype(np.float32).astype(dtype).astype(np.float64)
    return np.moveaxis((codes * scale).reshape(v.shape), -1, axis)


WIDE = False


def mx_kscale(k):
    if not WIDE:
        return np.ones(k)
    levels = np.array([10, -10, 5, -5, 0])
    if k % 512:
        return np.exp2(np.random.permutation(np.resize(levels, k // 32))).repeat(32)
    a = np.empty((k // 512, 16))
    for p in range(k // 512):
        a[p, :8] = np.random.permutation(np.resize(levels, 8))
        for g in range(8):
            far = levels[np.abs(levels - a[p, g]) >= 10]
            a[p, g + 8] = far[np.random.randint(len(far))]
    return np.exp2(a.ravel()).repeat(32)


def f64(x):
    return np.asarray(x).astype(np.float64)


def striped(idx):
    return np.tile(idx.reshape(-1, 16).T, (8, 1)).astype(np.uint16)


def unstriped(offs):
    return offs[:16].T.reshape(-1).astype(np.int64)


def pack_weight(w):
    k, n = w.shape
    w = f64(np.asarray(w, np.float32).astype(ml_dtypes.bfloat16)).reshape(k // 32, 32, n)
    amax = np.abs(w).max(1)
    byte = np.clip(np.where(amax > 0, np.frexp(amax)[1] - 1 + 127 - 7, 1), 1, 254)
    scaled = (w * np.exp2(127.0 - byte)[:, None, :]).reshape(k, n).astype(np.float32)
    words = np.ascontiguousarray(scaled.reshape(k // 512, 128, 4, n).transpose(0, 1, 3, 2)).astype(ml_dtypes.float8_e4m3fn).view(np.uint8)
    return words, np.ascontiguousarray(byte.astype(np.uint8).reshape(k // 512, 16, n))


def unpack_weight(words, scales):
    g, p, n, _ = words.shape
    vals = np.ascontiguousarray(words).view(ml_dtypes.float8_e4m3fn).astype(np.float64) * np.repeat(np.exp2(scales.astype(np.float64) - 127.0), 8, axis=1)[..., None]
    return vals.transpose(0, 1, 3, 2).reshape(g * 512, n)


H, K, T, S, N = 512, 512, 2048, 512, 128
P = 2 ** 7


def setup_inputs():
    n = np.random.standard_normal
    s = mx_kscale(K)[:, None]
    u = mx_kscale(H)
    packed_xT = pack_weight(n((K, T)) * s)
    packed_eT = pack_weight(n((K, T)) * s)
    return {
        "x_words": packed_xT[0],
        "x_scales": packed_xT[1],
        "e_words": packed_eT[0],
        "e_scales": packed_eT[1],
        "w1": (n((K, H)) / np.sqrt(K) / s).astype(np.float32),
        "unit": (np.random.uniform(0.5, 1.5, (H, 1)) * u[:, None]).astype(np.float32),
        "w2": (n((H, N)) / np.sqrt(2 * H) / u[:, None]).astype(np.float32),
        "w3": (n((H, N)) / np.sqrt(2 * H) / u[:, None]).astype(np.float32),
        "half": (np.tile(np.random.uniform(0.4, 0.6, S), (P, 1))).astype(np.float32),
        "offs": striped(np.random.permutation(T)[:S]),
    }


def reference(x_words, x_scales, e_words, e_scales, w1, unit, w2, w3, half, offs):
    xq = unpack_weight(x_words, x_scales)[:, unstriped(offs)]
    w1q = mxq(f64(w1), 0, "e4m3")
    hid = np.tanh(w1q.T @ xq)
    slo = -1.0 * ((hid) ** 2) + 1.0
    e_offs = unpack_weight(e_words, e_scales)[:, unstriped(offs)]
    tan = w1q.T @ e_offs
    done = slo * tan
    zone = f64(unit) * done
    fd = mxq(f64(w2), 0, "e4m3").T @ mxq(zone, 0, "e4m3")
    ztwo = f64(unit) * ((hid * done) * tan)
    return ((fd) ** 2) * f64(half)[:1] - ((mxq(f64(w3), 0, "e4m3").T @ mxq(ztwo, 0, "e4m3")))

@@ -1,0 +1,220 @@
+from contextlib import ExitStack
+
+import concourse.mybir as mybir
+
+K, H, T, S, N = 512, 512, 2048, 512, 128
+FLOPS = 2 * (2 * K * H * S + 2 * H * N * S)
+
+F32 = mybir.dt.float32
+BF16 = mybir.dt.bfloat16
+I32 = mybir.dt.int32
+U32 = mybir.dt.uint32
+U16 = mybir.dt.uint16
+U8 = mybir.dt.uint8
+FP8X4 = mybir.dt.float8_e4m3fn_x4
+ACT = mybir.ActivationFunctionType
+ALU = mybir.AluOpType
+
+P = 128
+PACK = 4
+CHUNK = 128
+CHUNKS = S // CHUNK
+PICK = 256
+E_ROW = 4
+
+
+def tile_picked_yjvptn_sec_p_kernel(tc, x_words, x_scales, e_words, e_scales, w1, unit, w2, w3, half, offs, out):
+    nc = tc.nc
+    with ExitStack() as ctx:
+        keep = ctx.enter_context(tc.tile_pool(name="keep", bufs=1))
+        psum = ctx.enter_context(tc.psum_pool(name="psum", bufs=1))
+
+        def sb(name, width, dtype):
+            return keep.tile([P, width], dtype, name=name, align_bytes=64)
+
+        offsets = keep.tile([P, S // 16], U16, name="offsets")
+        x_table = sb("x_table", T, I32)
+        e_table = sb("e_table", T, I32)
+        x_scale_table = sb("x_scale_table", T, U8)
+        e_scale_table = sb("e_scale_table", T, U8)
+        nc.gpsimd.memset(x_scale_table[:].bitcast(I32), 0)
+        nc.vector.memset(e_scale_table[:].bitcast(I32), 0)
+
+        unit_sb = sb("unit_sb", PACK, F32)
+        w1_raw = [keep.tile([P, PACK, H // 2], F32, name="w1_raw%d" % i, align_bytes=64) for i in range(2)]
+        w_raw = [keep.tile([P, PACK, N], F32, name="w_raw%d" % i, align_bytes=64) for i in range(2)]
+        half_sb = sb("half_sb", S, F32)
+
+        def load_scales(table, scales, row):
+            for q in range(4):
+                nc.sync.dma_start(out=table[32 * q + row : 32 * q + row + 4, :].bitcast(I32), in_=scales[0, 4 * q : 4 * q + 4, :].bitcast(I32))
+
+        def load_words(table, words):
+            nc.sync.dma_start(out=table[:], in_=words[0].rearrange("p n t -> p (n t)").bitcast(I32))
+
+        w1_rows = w1.rearrange("(p j) c -> p j c", j=PACK)
+        nc.sync.dma_start(offsets[:], offs)
+        load_scales(x_scale_table, x_scales, 0)
+        for i in range(2):
+            nc.sync.dma_start(out=w1_raw[i][:], in_=w1_rows[:, :, i * (H // 2) : (i + 1) * (H // 2)])
+        load_words(x_table, x_words)
+        load_scales(e_scale_table, e_scales, E_ROW)
+        nc.sync.dma_start(out=unit_sb[:], in_=unit.rearrange("(p t) o -> p (t o)", t=PACK))
+        load_words(e_table, e_words)
+        for raw, w in zip(w_raw, (w2, w3)):
+            nc.sync.dma_start(out=raw[:], in_=w.rearrange("(p j) n -> p j n", j=PACK))
+        nc.sync.dma_start(out=half_sb[:], in_=half)
+
+        w1_bf = sb("w1_bf", PACK * H, BF16)
+        w1_dealt = w1_bf[:].rearrange("p (t m j) -> p m j t", t=PACK, j=PACK)
+        nc.scalar.copy(w1_dealt[:, 0:64], w1_raw[0][:].rearrange("p j (m t) -> p m j t", t=PACK))
+        nc.vector.tensor_copy(w1_dealt[:, 64:128], w1_raw[1][:].rearrange("p j (m t) -> p m j t", t=PACK))
+        w1_codes = sb("w1_codes", H, U32)
+        w1_scale = sb("w1_scale", H, U8)
+        nc.vector.quantize_mx(out=w1_codes[:].bitcast(FP8X4), scales=w1_scale[:], in_=w1_bf[:])
+
+        x_scale = sb("x_scale", S, U8)
+        e_scale = sb("e_scale", S, U8)
+        nc.vector.tensor_copy(x_scale[:], x_scale_table[:].indirect(offsets[:]))
+        neg_unit = sb("neg_unit", PACK, F32)
+        nc.vector.tensor_scalar(neg_unit[:], unit_sb[:], -1.0, None, ALU.mult)
+
+        def pick(name, table, g):
+            codes = sb("%s_codes%d" % (name, g), PICK, U32)
+            nc.vector.tensor_copy(codes[:], table[:].bitcast(U32).indirect(offsets[:, g * PICK // 16 : (g + 1) * PICK // 16]))
+            return codes
+
+        def first_product(tag, c, codes, scale, row):
+            bank = psum.tile([P, PACK, CHUNK], F32, name="%s%d" % (tag, c), tag="%s%d" % (tag, c))
+            lo = (c * CHUNK) % PICK
+            for t in range(PACK):
+                nc.tensor.matmul_mx(
+                    out=bank[:, t, :],
+                    lhsT=w1_codes[:, t * P : (t + 1) * P].bitcast(FP8X4),
+                    lhsT_scale=w1_scale[:, t * P : (t + 1) * P],
+                    rhs=codes[:, lo : lo + CHUNK].bitcast(FP8X4),
+                    rhs_scale=scale[row:P, c * CHUNK : (c + 1) * CHUNK],
+                    start=True,
+                    stop=True,
+                )
+            return bank[:].rearrange("p t n -> p (t n)")
+
+        W = PACK * CHUNK
+        x_codes = [pick("x", x_table, g) for g in range(S // PICK)]
+        pre = [first_product("a", c, x_codes[c * CHUNK // PICK], x_scale, 0) for c in range(CHUNKS)]
+        nc.vector.tensor_copy(e_scale[:], e_scale_table[:].indirect(offsets[:]))
+        e_codes = [pick("e", e_table, g) for g in range(S // PICK)]
+        tan = [first_product("b", c, e_codes[c * CHUNK // PICK], e_scale, E_ROW) for c in range(CHUNKS)]
+
+        HALVES = S // PICK
+        hid = [keep.tile([P, PACK, PICK], F32, name="hid%d" % g) for g in range(HALVES)]
+        hsq = [keep.tile([P, PACK, PICK], F32, name="hsq%d" % g) for g in range(HALVES)]
+        slope = [keep.tile([P, PACK, PICK], F32, name="slope%d" % g) for g in range(HALVES)]
+        zone = [sb("zone%d" % c, W, F32) for c in range(CHUNKS)]
+        htan = [sb("htan%d" % c, W, F32) for c in range(CHUNKS)]
+        groups = [(0, 2), (2, 1), (3, 1)]
+        z_bf = [{first: sb("z_bf%d_%d" % (i, first), n * W, BF16) for first, n in groups} for i in range(2)]
+        w_bf = sb("w_bf", 2 * PACK * N, BF16)
+        w_codes = sb("w_codes", 2 * N, U32)
+        w_scale = sb("w_scale", 2 * N, U8)
+
+        def planar(ap):
+            return ap.rearrange("p (t g i) -> p g t i", t=PACK, i=4)
+
+        def woven(ap):
+            return ap.rearrange("p (g i t) -> p g t i", t=PACK, i=4)
+
+        def part(tiles, c):
+            lo = (c * CHUNK) % PICK
+            return tiles[c * CHUNK // PICK][:, :, lo : lo + CHUNK]
+
+        def by_t(ap):
+            return ap.rearrange("p (t n) -> p t n", t=PACK)
+
+        def z_part(i, c):
+            first = max(f for f, n in groups if f <= c)
+            return woven(z_bf[i][first][:, (c - first) * W : (c - first + 1) * W])
+
+        def hidden(c):
+            nc.scalar.activation(part(hid, c), by_t(pre[c]), ACT.Tanh)
+
+        def square(g):
+            nc.scalar.activation(hsq[g][:], hid[g][:], ACT.Square)
+
+        def slopes(g):
+            for t in range(PACK):
+                nc.scalar.activation(slope[g][:, t, :], hsq[g][:, t, :], ACT.Identity, bias=unit_sb[:, t : t + 1], scale=neg_unit[:, t : t + 1])
+
+        def make_htan(c):
+            nc.vector.tensor_tensor(by_t(htan[c][:]), by_t(tan[c]), part(hid, c), ALU.mult)
+
+        def make_zone(c):
+            nc.vector.tensor_tensor(by_t(zone[c][:]), by_t(tan[c]), part(slope, c), ALU.mult)
+
+        def round_zone(c):
+            nc.scalar.copy(z_part(0, c), planar(zone[c][:]))
+
+        def make_ztwo(c):
+            nc.vector.tensor_tensor(z_part(1, c), planar(zone[c][:]), planar(htan[c][:]), ALU.mult)
+
+        def second_weights():
+            for i in range(2):
+                nc.scalar.copy(woven(w_bf[:, i * PACK * N : (i + 1) * PACK * N]), planar(w_raw[i][:].rearrange("p j n -> p (j n)")))
+            nc.vector.quantize_mx(out=w_codes[:].bitcast(FP8X4), scales=w_scale[:], in_=w_bf[:])
+
+        def second_product(i, tag, first, n):
+            codes = sb("z_codes%d_%d" % (i, first), n * CHUNK, U32)
+            scale = sb("z_scale%d_%d" % (i, first), n * CHUNK, U8)
+            nc.vector.quantize_mx(out=codes[:].bitcast(FP8X4), scales=scale[:], in_=z_bf[i][first][:])
+            bank = psum.tile([P, n * CHUNK], F32, name="%s%d" % (tag, first), tag="%s%d" % (tag, first))
+            nc.tensor.matmul_mx(
+                out=bank[:],
+                lhsT=w_codes[:, i * N : (i + 1) * N].bitcast(FP8X4),
+                lhsT_scale=w_scale[:, i * N : (i + 1) * N],
+                rhs=codes[:].bitcast(FP8X4),
+                rhs_scale=scale[:],
+                start=True,
+                stop=True,
+            )
+            return bank
+
+        def multiply(first, n):
+            fd = second_product(0, "a", first, n)
+            fd_sq = sb("fd_sq%d" % first, n * CHUNK, F32)
+            nc.scalar.activation(fd_sq[:], fd[:], ACT.Square)
+            return fd_sq, second_product(1, "b", first, n)
+
+        def finish(first, n, fd_sq, curve):
+            cols = slice(first * CHUNK, (first + n) * CHUNK)
+            weighted = sb("weighted%d" % first, n * CHUNK, F32)
+            result = sb("result%d" % first, n * CHUNK, F32)
+            nc.vector.tensor_tensor(weighted[:], fd_sq[:], half_sb[:, cols], ALU.mult)
+            nc.vector.tensor_tensor(result[:], weighted[:], curve[:], ALU.subtract)
+            nc.sync.dma_start(out=out[:, cols], in_=result[:])
+
+        hidden(0)
+        hidden(1)
+        hidden(2)
+        square(0)
+        hidden(3)
+        slopes(0)
+        square(1)
+        slopes(1)
+        for c in range(CHUNKS):
+            make_htan(c)
+        for c in range(CHUNKS):
+            make_zone(c)
+        round_zone(0)
+        round_zone(1)
+        second_weights()
+        round_zone(2)
+        round_zone(3)
+        for c in range(3):
+            make_ztwo(c)
+        done0 = multiply(*groups[0])
+        make_ztwo(3)
+        done1 = multiply(*groups[1])
+        done2 = multiply(*groups[2])
+        finish(*groups[0], *done0)
+        finish(*groups[1], *done1)
+        finish(*groups[2], *done2)

@@ -17,10 +17,17 @@ ALU = mybir.AluOpType
 
 P = 128
 PACK = 4
+LIST_ROWS = 16
+QUADRANT = 32
+SCALE_ROWS = 4
 CHUNK = 128
 CHUNKS = S // CHUNK
-PICK = 256
-E_ROW = 4
+BANK = PACK * CHUNK
+HALF = 256
+HALVES = S // HALF
+PER_HALF = HALF // CHUNK
+X_ROW, E_ROW = 0, 4
+COPY_RUN, PRODUCT_RUN = 4, 2
 
 
 def tile_picked_yjvptn_sec_p_kernel(tc, x_words, x_scales, e_words, e_scales, w1, unit, w2, w3, half, offs, out):
@@ -32,7 +39,7 @@ def tile_picked_yjvptn_sec_p_kernel(tc, x_words, x_scales, e_words, e_scales, w1
         def sb(name, width, dtype):
             return keep.tile([P, width], dtype, name=name, align_bytes=64)
 
-        offsets = keep.tile([P, S // 16], U16, name="offsets")
+        offsets = keep.tile([P, S // LIST_ROWS], U16, name="offsets")
         x_table = sb("x_table", T, I32)
         e_table = sb("e_table", T, I32)
         x_scale_table = sb("x_scale_table", T, U8)
@@ -41,34 +48,38 @@ def tile_picked_yjvptn_sec_p_kernel(tc, x_words, x_scales, e_words, e_scales, w1
         nc.vector.memset(e_scale_table[:].bitcast(I32), 0)
 
         unit_sb = sb("unit_sb", PACK, F32)
-        w1_raw = [keep.tile([P, PACK, H // 2], F32, name="w1_raw%d" % i, align_bytes=64) for i in range(2)]
-        w_raw = [keep.tile([P, PACK, N], F32, name="w_raw%d" % i, align_bytes=64) for i in range(2)]
+        w1_raw = [keep.tile([P, PACK // 2, H], F32, name="w1_raw%d" % i, align_bytes=64) for i in range(2)]
+        w23_raw = [keep.tile([P, PACK, N], F32, name="w23_raw%d" % i, align_bytes=64) for i in range(2)]
         half_sb = sb("half_sb", S, F32)
 
         def load_scales(table, scales, row):
-            for q in range(4):
-                nc.sync.dma_start(out=table[32 * q + row : 32 * q + row + 4, :].bitcast(I32), in_=scales[0, 4 * q : 4 * q + 4, :].bitcast(I32))
+            for q in (0, 2, 1, 3):
+                first = QUADRANT * q + row
+                nc.sync.dma_start(
+                    out=table[first : first + SCALE_ROWS, :].bitcast(I32),
+                    in_=scales[0, SCALE_ROWS * q : SCALE_ROWS * (q + 1), :].bitcast(I32),
+                )
 
         def load_words(table, words):
             nc.sync.dma_start(out=table[:], in_=words[0].rearrange("p n t -> p (n t)").bitcast(I32))
 
         w1_rows = w1.rearrange("(p j) c -> p j c", j=PACK)
+        nc.sync.dma_start(out=w1_raw[0][:], in_=w1_rows[:, 0:2, :])
         nc.sync.dma_start(offsets[:], offs)
-        load_scales(x_scale_table, x_scales, 0)
-        for i in range(2):
-            nc.sync.dma_start(out=w1_raw[i][:], in_=w1_rows[:, :, i * (H // 2) : (i + 1) * (H // 2)])
+        load_scales(x_scale_table, x_scales, X_ROW)
+        nc.sync.dma_start(out=w1_raw[1][:], in_=w1_rows[:, 2:4, :])
         load_words(x_table, x_words)
-        load_scales(e_scale_table, e_scales, E_ROW)
         nc.sync.dma_start(out=unit_sb[:], in_=unit.rearrange("(p t) o -> p (t o)", t=PACK))
+        load_scales(e_scale_table, e_scales, E_ROW)
         load_words(e_table, e_words)
-        for raw, w in zip(w_raw, (w2, w3)):
-            nc.sync.dma_start(out=raw[:], in_=w.rearrange("(p j) n -> p j n", j=PACK))
         nc.sync.dma_start(out=half_sb[:], in_=half)
+        for raw, w in zip(w23_raw, (w2, w3)):
+            nc.sync.dma_start(out=raw[:], in_=w.rearrange("(p j) n -> p j n", j=PACK))
 
         w1_bf = sb("w1_bf", PACK * H, BF16)
         w1_dealt = w1_bf[:].rearrange("p (t m j) -> p m j t", t=PACK, j=PACK)
-        nc.scalar.copy(w1_dealt[:, 0:64], w1_raw[0][:].rearrange("p j (m t) -> p m j t", t=PACK))
-        nc.vector.tensor_copy(w1_dealt[:, 64:128], w1_raw[1][:].rearrange("p j (m t) -> p m j t", t=PACK))
+        nc.scalar.copy(w1_dealt[:, :, 0:2, :], w1_raw[0][:].rearrange("p j (m t) -> p m j t", t=PACK))
+        nc.vector.tensor_copy(w1_dealt[:, :, 2:4, :], w1_raw[1][:].rearrange("p j (m t) -> p m j t", t=PACK))
         w1_codes = sb("w1_codes", H, U32)
         w1_scale = sb("w1_scale", H, U8)
         nc.vector.quantize_mx(out=w1_codes[:].bitcast(FP8X4), scales=w1_scale[:], in_=w1_bf[:])
@@ -80,97 +91,91 @@ def tile_picked_yjvptn_sec_p_kernel(tc, x_words, x_scales, e_words, e_scales, w1
         nc.vector.tensor_scalar(neg_unit[:], unit_sb[:], -1.0, None, ALU.mult)
 
         def pick(name, table, g):
-            codes = sb("%s_codes%d" % (name, g), PICK, U32)
-            nc.vector.tensor_copy(codes[:], table[:].bitcast(U32).indirect(offsets[:, g * PICK // 16 : (g + 1) * PICK // 16]))
+            codes = sb("%s_codes%d" % (name, g), HALF, U32)
+            entries = offsets[:, g * HALF // LIST_ROWS : (g + 1) * HALF // LIST_ROWS]
+            nc.vector.tensor_copy(codes[:], table[:].bitcast(U32).indirect(entries))
             return codes
 
         def first_product(tag, c, codes, scale, row):
             bank = psum.tile([P, PACK, CHUNK], F32, name="%s%d" % (tag, c), tag="%s%d" % (tag, c))
-            lo = (c * CHUNK) % PICK
+            lo = (c % PER_HALF) * CHUNK
             for t in range(PACK):
                 nc.tensor.matmul_mx(
                     out=bank[:, t, :],
                     lhsT=w1_codes[:, t * P : (t + 1) * P].bitcast(FP8X4),
                     lhsT_scale=w1_scale[:, t * P : (t + 1) * P],
-                    rhs=codes[:, lo : lo + CHUNK].bitcast(FP8X4),
+                    rhs=codes[c // PER_HALF][:, lo : lo + CHUNK].bitcast(FP8X4),
                     rhs_scale=scale[row:P, c * CHUNK : (c + 1) * CHUNK],
                     start=True,
                     stop=True,
                 )
-            return bank[:].rearrange("p t n -> p (t n)")
+            return bank[:]
 
-        W = PACK * CHUNK
-        x_codes = [pick("x", x_table, g) for g in range(S // PICK)]
-        pre = [first_product("a", c, x_codes[c * CHUNK // PICK], x_scale, 0) for c in range(CHUNKS)]
+        x_codes = [pick("x", x_table, g) for g in range(HALVES)]
+        pre = [first_product("x_bank", c, x_codes, x_scale, X_ROW) for c in range(CHUNKS)]
         nc.vector.tensor_copy(e_scale[:], e_scale_table[:].indirect(offsets[:]))
-        e_codes = [pick("e", e_table, g) for g in range(S // PICK)]
-        tan = [first_product("b", c, e_codes[c * CHUNK // PICK], e_scale, E_ROW) for c in range(CHUNKS)]
+        e_codes = [pick("e", e_table, g) for g in range(HALVES)]
+        tan = [first_product("e_bank", c, e_codes, e_scale, E_ROW) for c in range(CHUNKS)]
 
-        HALVES = S // PICK
-        hid = [keep.tile([P, PACK, PICK], F32, name="hid%d" % g) for g in range(HALVES)]
-        hsq = [keep.tile([P, PACK, PICK], F32, name="hsq%d" % g) for g in range(HALVES)]
-        slope = [keep.tile([P, PACK, PICK], F32, name="slope%d" % g) for g in range(HALVES)]
-        zone = [sb("zone%d" % c, W, F32) for c in range(CHUNKS)]
-        htan = [sb("htan%d" % c, W, F32) for c in range(CHUNKS)]
-        groups = [(0, 2), (2, 1), (3, 1)]
-        z_bf = [{first: sb("z_bf%d_%d" % (i, first), n * W, BF16) for first, n in groups} for i in range(2)]
-        w_bf = sb("w_bf", 2 * PACK * N, BF16)
-        w_codes = sb("w_codes", 2 * N, U32)
-        w_scale = sb("w_scale", 2 * N, U8)
+        hid = [keep.tile([P, PACK, HALF], F32, name="hid%d" % g) for g in range(HALVES)]
+        hid_sq = [keep.tile([P, PACK, HALF], F32, name="hid_sq%d" % g) for g in range(HALVES)]
+        slope = [keep.tile([P, PACK, HALF], F32, name="slope%d" % g) for g in range(HALVES)]
+        zone = [sb("zone%d" % c, BANK, F32) for c in range(CHUNKS)]
+        hid_tan = [sb("hid_tan%d" % c, BANK, F32) for c in range(CHUNKS)]
+        zone_bf = [sb("zone_bf%d" % g, PACK * HALF, BF16) for g in range(HALVES)]
+        ztwo_bf = [sb("ztwo_bf%d" % g, PACK * HALF, BF16) for g in range(HALVES)]
+        w23_bf = sb("w23_bf", 2 * PACK * N, BF16)
+        w23_codes = sb("w23_codes", 2 * N, U32)
+        w23_scale = sb("w23_scale", 2 * N, U8)
+        fd_sq, curve, weighted = {}, {}, {}
 
-        def planar(ap):
-            return ap.rearrange("p (t g i) -> p g t i", t=PACK, i=4)
+        def chunk_of(halves, c):
+            lo = (c % PER_HALF) * CHUNK
+            return halves[c // PER_HALF][:, :, lo : lo + CHUNK]
 
-        def woven(ap):
-            return ap.rearrange("p (g i t) -> p g t i", t=PACK, i=4)
+        def by_plane(tile):
+            return tile[:].rearrange("p (t n) -> p t n", t=PACK)
 
-        def part(tiles, c):
-            lo = (c * CHUNK) % PICK
-            return tiles[c * CHUNK // PICK][:, :, lo : lo + CHUNK]
+        def planar(tile, run):
+            return tile[:].rearrange("p (t g i) -> p g t i", t=PACK, i=run)
 
-        def by_t(ap):
-            return ap.rearrange("p (t n) -> p t n", t=PACK)
+        def woven(halves, c, run):
+            lo = (c % PER_HALF) * BANK
+            return halves[c // PER_HALF][:, lo : lo + BANK].rearrange("p (g i t) -> p g t i", t=PACK, i=run)
 
-        def z_part(i, c):
-            first = max(f for f, n in groups if f <= c)
-            return woven(z_bf[i][first][:, (c - first) * W : (c - first + 1) * W])
+        def make_hid(c):
+            nc.scalar.activation(chunk_of(hid, c), pre[c], ACT.Tanh)
 
-        def hidden(c):
-            nc.scalar.activation(part(hid, c), by_t(pre[c]), ACT.Tanh)
+        def make_hid_sq(g):
+            nc.scalar.activation(hid_sq[g][:], hid[g][:], ACT.Square)
 
-        def square(g):
-            nc.scalar.activation(hsq[g][:], hid[g][:], ACT.Square)
-
-        def slopes(g):
+        def make_slope(g):
             for t in range(PACK):
-                nc.scalar.activation(slope[g][:, t, :], hsq[g][:, t, :], ACT.Identity, bias=unit_sb[:, t : t + 1], scale=neg_unit[:, t : t + 1])
+                nc.scalar.activation(
+                    slope[g][:, t, :], hid_sq[g][:, t, :], ACT.Identity, bias=unit_sb[:, t : t + 1], scale=neg_unit[:, t : t + 1]
+                )
 
-        def make_htan(c):
-            nc.vector.tensor_tensor(by_t(htan[c][:]), by_t(tan[c]), part(hid, c), ALU.mult)
+        def make_hid_tan(c):
+            nc.vector.tensor_tensor(by_plane(hid_tan[c]), tan[c], chunk_of(hid, c), ALU.mult)
 
         def make_zone(c):
-            nc.vector.tensor_tensor(by_t(zone[c][:]), by_t(tan[c]), part(slope, c), ALU.mult)
+            nc.vector.tensor_tensor(by_plane(zone[c]), tan[c], chunk_of(slope, c), ALU.mult)
 
         def round_zone(c):
-            nc.scalar.copy(z_part(0, c), planar(zone[c][:]))
+            nc.scalar.copy(woven(zone_bf, c, COPY_RUN), planar(zone[c], COPY_RUN))
 
         def make_ztwo(c):
-            nc.vector.tensor_tensor(z_part(1, c), planar(zone[c][:]), planar(htan[c][:]), ALU.mult)
+            nc.vector.tensor_tensor(woven(ztwo_bf, c, PRODUCT_RUN), planar(zone[c], PRODUCT_RUN), planar(hid_tan[c], PRODUCT_RUN), ALU.mult)
 
-        def second_weights():
-            for i in range(2):
-                nc.scalar.copy(woven(w_bf[:, i * PACK * N : (i + 1) * PACK * N]), planar(w_raw[i][:].rearrange("p j n -> p (j n)")))
-            nc.vector.quantize_mx(out=w_codes[:].bitcast(FP8X4), scales=w_scale[:], in_=w_bf[:])
-
-        def second_product(i, tag, first, n):
-            codes = sb("z_codes%d_%d" % (i, first), n * CHUNK, U32)
-            scale = sb("z_scale%d_%d" % (i, first), n * CHUNK, U8)
-            nc.vector.quantize_mx(out=codes[:].bitcast(FP8X4), scales=scale[:], in_=z_bf[i][first][:])
-            bank = psum.tile([P, n * CHUNK], F32, name="%s%d" % (tag, first), tag="%s%d" % (tag, first))
+        def second_product(i, tag, values, g):
+            codes = sb("z_codes%d_%d" % (i, g), HALF, U32)
+            scale = sb("z_scale%d_%d" % (i, g), HALF, U8)
+            nc.vector.quantize_mx(out=codes[:].bitcast(FP8X4), scales=scale[:], in_=values[g][:])
+            bank = psum.tile([P, HALF], F32, name="second%d_%d" % (i, g), tag="%s%d" % (tag, g * PER_HALF))
             nc.tensor.matmul_mx(
                 out=bank[:],
-                lhsT=w_codes[:, i * N : (i + 1) * N].bitcast(FP8X4),
-                lhsT_scale=w_scale[:, i * N : (i + 1) * N],
+                lhsT=w23_codes[:, i * N : (i + 1) * N].bitcast(FP8X4),
+                lhsT_scale=w23_scale[:, i * N : (i + 1) * N],
                 rhs=codes[:].bitcast(FP8X4),
                 rhs_scale=scale[:],
                 start=True,
@@ -178,43 +183,60 @@ def tile_picked_yjvptn_sec_p_kernel(tc, x_words, x_scales, e_words, e_scales, w1
             )
             return bank
 
-        def multiply(first, n):
-            fd = second_product(0, "a", first, n)
-            fd_sq = sb("fd_sq%d" % first, n * CHUNK, F32)
-            nc.scalar.activation(fd_sq[:], fd[:], ACT.Square)
-            return fd_sq, second_product(1, "b", first, n)
+        def make_fd_sq(g):
+            fd = second_product(0, "x_bank", zone_bf, g)
+            fd_sq[g] = sb("fd_sq%d" % g, HALF, F32)
+            nc.scalar.activation(fd_sq[g][:], fd[:], ACT.Square)
 
-        def finish(first, n, fd_sq, curve):
-            cols = slice(first * CHUNK, (first + n) * CHUNK)
-            weighted = sb("weighted%d" % first, n * CHUNK, F32)
-            result = sb("result%d" % first, n * CHUNK, F32)
-            nc.vector.tensor_tensor(weighted[:], fd_sq[:], half_sb[:, cols], ALU.mult)
-            nc.vector.tensor_tensor(result[:], weighted[:], curve[:], ALU.subtract)
-            nc.sync.dma_start(out=out[:, cols], in_=result[:])
+        def make_curve(g):
+            curve[g] = second_product(1, "e_bank", ztwo_bf, g)
 
-        hidden(0)
-        hidden(1)
-        hidden(2)
-        square(0)
-        hidden(3)
-        slopes(0)
-        square(1)
-        slopes(1)
+        def weigh(g):
+            weighted[g] = sb("weighted%d" % g, HALF, F32)
+            nc.vector.tensor_tensor(weighted[g][:], fd_sq[g][:], half_sb[:, g * HALF : (g + 1) * HALF], ALU.mult)
+
+        def finish(g):
+            result = sb("result%d" % g, HALF, F32)
+            nc.vector.tensor_tensor(result[:], weighted[g][:], curve[g][:], ALU.subtract)
+            nc.sync.dma_start(out=out[:, g * HALF : (g + 1) * HALF], in_=result[:])
+
+        for c in range(PER_HALF + 1):
+            make_hid(c)
+        make_hid_sq(0)
+        make_hid(CHUNKS - 1)
+        make_slope(0)
+        make_hid_sq(1)
+        make_slope(1)
+
+        for i in range(2):
+            nc.gpsimd.tensor_scalar(
+                w23_bf[:, i * PACK * N : (i + 1) * PACK * N].rearrange("p (n j) -> p n j", j=PACK),
+                w23_raw[i][:].rearrange("p j n -> p n j"),
+                1.0,
+                0.0,
+                ALU.mult,
+                ALU.add,
+            )
+
         for c in range(CHUNKS):
-            make_htan(c)
-        for c in range(CHUNKS):
+            make_hid_tan(c)
+        for c in range(PER_HALF):
             make_zone(c)
-        round_zone(0)
-        round_zone(1)
-        second_weights()
-        round_zone(2)
-        round_zone(3)
-        for c in range(3):
+        nc.vector.quantize_mx(out=w23_codes[:].bitcast(FP8X4), scales=w23_scale[:], in_=w23_bf[:])
+        for c in range(PER_HALF):
             make_ztwo(c)
-        done0 = multiply(*groups[0])
-        make_ztwo(3)
-        done1 = multiply(*groups[1])
-        done2 = multiply(*groups[2])
-        finish(*groups[0], *done0)
-        finish(*groups[1], *done1)
-        finish(*groups[2], *done2)
+        for c in range(PER_HALF, CHUNKS):
+            make_zone(c)
+        for c in range(CHUNKS):
+            round_zone(c)
+
+        make_fd_sq(0)
+        make_curve(0)
+        make_ztwo(CHUNKS - 2)
+        make_fd_sq(1)
+        make_ztwo(CHUNKS - 1)
+        weigh(0)
+        make_curve(1)
+        weigh(1)
+        for g in range(HALVES):
+            finish(g)

from contextlib import ExitStack

import concourse.mybir as mybir

K, H, T, S, N = 512, 512, 2048, 512, 128
FLOPS = 2 * (2 * K * H * S + 2 * H * N * S)

F32 = mybir.dt.float32
BF16 = mybir.dt.bfloat16
I32 = mybir.dt.int32
U32 = mybir.dt.uint32
U16 = mybir.dt.uint16
U8 = mybir.dt.uint8
FP8X4 = mybir.dt.float8_e4m3fn_x4
ACT = mybir.ActivationFunctionType
ALU = mybir.AluOpType

P = 128
PACK = 4
LIST_ROWS = 16
QUADRANT = 32
SCALE_ROWS = 4
CHUNK = 128
CHUNKS = S // CHUNK
BANK = PACK * CHUNK
HALF = 256
HALVES = S // HALF
PER_HALF = HALF // CHUNK
X_ROW, E_ROW = 0, 4
COPY_RUN, PRODUCT_RUN = 4, 2


def tile_picked_yjvptn_sec_p_kernel(tc, x_words, x_scales, e_words, e_scales, w1, unit, w2, w3, half, offs, out):
    nc = tc.nc
    with ExitStack() as ctx:
        keep = ctx.enter_context(tc.tile_pool(name="keep", bufs=1))
        psum = ctx.enter_context(tc.psum_pool(name="psum", bufs=1))

        def sb(name, width, dtype):
            return keep.tile([P, width], dtype, name=name, align_bytes=64)

        offsets = keep.tile([P, S // LIST_ROWS], U16, name="offsets")
        x_table = sb("x_table", T, I32)
        e_table = sb("e_table", T, I32)
        x_scale_table = sb("x_scale_table", T, U8)
        e_scale_table = sb("e_scale_table", T, U8)
        nc.gpsimd.memset(x_scale_table[:].bitcast(I32), 0)
        nc.vector.memset(e_scale_table[:].bitcast(I32), 0)

        unit_sb = sb("unit_sb", PACK, F32)
        w1_raw = [keep.tile([P, PACK // 2, H], F32, name="w1_raw%d" % i, align_bytes=64) for i in range(2)]
        w23_raw = [keep.tile([P, PACK, N], F32, name="w23_raw%d" % i, align_bytes=64) for i in range(2)]
        half_sb = sb("half_sb", S, F32)

        def load_scales(table, scales, row):
            for q in (0, 2, 1, 3):
                first = QUADRANT * q + row
                nc.sync.dma_start(
                    out=table[first : first + SCALE_ROWS, :].bitcast(I32),
                    in_=scales[0, SCALE_ROWS * q : SCALE_ROWS * (q + 1), :].bitcast(I32),
                )

        def load_words(table, words):
            nc.sync.dma_start(out=table[:], in_=words[0].rearrange("p n t -> p (n t)").bitcast(I32))

        w1_rows = w1.rearrange("(p j) c -> p j c", j=PACK)
        nc.sync.dma_start(out=w1_raw[0][:], in_=w1_rows[:, 0:2, :])
        nc.sync.dma_start(offsets[:], offs)
        load_scales(x_scale_table, x_scales, X_ROW)
        nc.sync.dma_start(out=w1_raw[1][:], in_=w1_rows[:, 2:4, :])
        load_words(x_table, x_words)
        nc.sync.dma_start(out=unit_sb[:], in_=unit.rearrange("(p t) o -> p (t o)", t=PACK))
        load_scales(e_scale_table, e_scales, E_ROW)
        load_words(e_table, e_words)
        nc.sync.dma_start(out=half_sb[:], in_=half)
        for raw, w in zip(w23_raw, (w2, w3)):
            nc.sync.dma_start(out=raw[:], in_=w.rearrange("(p j) n -> p j n", j=PACK))

        w1_bf = sb("w1_bf", PACK * H, BF16)
        w1_dealt = w1_bf[:].rearrange("p (t m j) -> p m j t", t=PACK, j=PACK)
        nc.scalar.copy(w1_dealt[:, :, 0:2, :], w1_raw[0][:].rearrange("p j (m t) -> p m j t", t=PACK))
        nc.vector.tensor_copy(w1_dealt[:, :, 2:4, :], w1_raw[1][:].rearrange("p j (m t) -> p m j t", t=PACK))
        w1_codes = sb("w1_codes", H, U32)
        w1_scale = sb("w1_scale", H, U8)
        nc.vector.quantize_mx(out=w1_codes[:].bitcast(FP8X4), scales=w1_scale[:], in_=w1_bf[:])

        x_scale = sb("x_scale", S, U8)
        e_scale = sb("e_scale", S, U8)
        nc.vector.tensor_copy(x_scale[:], x_scale_table[:].indirect(offsets[:]))
        neg_unit = sb("neg_unit", PACK, F32)
        nc.vector.tensor_scalar(neg_unit[:], unit_sb[:], -1.0, None, ALU.mult)

        def pick(name, table, g):
            codes = sb("%s_codes%d" % (name, g), HALF, U32)
            entries = offsets[:, g * HALF // LIST_ROWS : (g + 1) * HALF // LIST_ROWS]
            nc.vector.tensor_copy(codes[:], table[:].bitcast(U32).indirect(entries))
            return codes

        def first_product(tag, c, codes, scale, row):
            bank = psum.tile([P, PACK, CHUNK], F32, name="%s%d" % (tag, c), tag="%s%d" % (tag, c))
            lo = (c % PER_HALF) * CHUNK
            for t in range(PACK):
                nc.tensor.matmul_mx(
                    out=bank[:, t, :],
                    lhsT=w1_codes[:, t * P : (t + 1) * P].bitcast(FP8X4),
                    lhsT_scale=w1_scale[:, t * P : (t + 1) * P],
                    rhs=codes[c // PER_HALF][:, lo : lo + CHUNK].bitcast(FP8X4),
                    rhs_scale=scale[row:P, c * CHUNK : (c + 1) * CHUNK],
                    start=True,
                    stop=True,
                )
            return bank[:]

        x_codes = [pick("x", x_table, g) for g in range(HALVES)]
        pre = [first_product("x_bank", c, x_codes, x_scale, X_ROW) for c in range(CHUNKS)]
        nc.vector.tensor_copy(e_scale[:], e_scale_table[:].indirect(offsets[:]))
        e_codes = [pick("e", e_table, g) for g in range(HALVES)]
        tan = [first_product("e_bank", c, e_codes, e_scale, E_ROW) for c in range(CHUNKS)]

        hid = [keep.tile([P, PACK, HALF], F32, name="hid%d" % g) for g in range(HALVES)]
        hid_sq = [keep.tile([P, PACK, HALF], F32, name="hid_sq%d" % g) for g in range(HALVES)]
        slope = [keep.tile([P, PACK, HALF], F32, name="slope%d" % g) for g in range(HALVES)]
        zone = [sb("zone%d" % c, BANK, F32) for c in range(CHUNKS)]
        hid_tan = [sb("hid_tan%d" % c, BANK, F32) for c in range(CHUNKS)]
        zone_bf = [sb("zone_bf%d" % g, PACK * HALF, BF16) for g in range(HALVES)]
        ztwo_bf = [sb("ztwo_bf%d" % g, PACK * HALF, BF16) for g in range(HALVES)]
        w23_bf = sb("w23_bf", 2 * PACK * N, BF16)
        w23_codes = sb("w23_codes", 2 * N, U32)
        w23_scale = sb("w23_scale", 2 * N, U8)
        fd_sq, curve, weighted = {}, {}, {}

        def chunk_of(halves, c):
            lo = (c % PER_HALF) * CHUNK
            return halves[c // PER_HALF][:, :, lo : lo + CHUNK]

        def by_plane(tile):
            return tile[:].rearrange("p (t n) -> p t n", t=PACK)

        def planar(tile, run):
            return tile[:].rearrange("p (t g i) -> p g t i", t=PACK, i=run)

        def woven(halves, c, run):
            lo = (c % PER_HALF) * BANK
            return halves[c // PER_HALF][:, lo : lo + BANK].rearrange("p (g i t) -> p g t i", t=PACK, i=run)

        def make_hid(c):
            nc.scalar.activation(chunk_of(hid, c), pre[c], ACT.Tanh)

        def make_hid_sq(g):
            nc.scalar.activation(hid_sq[g][:], hid[g][:], ACT.Square)

        def make_slope(g):
            for t in range(PACK):
                nc.scalar.activation(
                    slope[g][:, t, :], hid_sq[g][:, t, :], ACT.Identity, bias=unit_sb[:, t : t + 1], scale=neg_unit[:, t : t + 1]
                )

        def make_hid_tan(c):
            nc.vector.tensor_tensor(by_plane(hid_tan[c]), tan[c], chunk_of(hid, c), ALU.mult)

        def make_zone(c):
            nc.vector.tensor_tensor(by_plane(zone[c]), tan[c], chunk_of(slope, c), ALU.mult)

        def round_zone(c):
            nc.scalar.copy(woven(zone_bf, c, COPY_RUN), planar(zone[c], COPY_RUN))

        def make_ztwo(c):
            nc.vector.tensor_tensor(woven(ztwo_bf, c, PRODUCT_RUN), planar(zone[c], PRODUCT_RUN), planar(hid_tan[c], PRODUCT_RUN), ALU.mult)

        def second_product(i, tag, values, g):
            codes = sb("z_codes%d_%d" % (i, g), HALF, U32)
            scale = sb("z_scale%d_%d" % (i, g), HALF, U8)
            nc.vector.quantize_mx(out=codes[:].bitcast(FP8X4), scales=scale[:], in_=values[g][:])
            bank = psum.tile([P, HALF], F32, name="second%d_%d" % (i, g), tag="%s%d" % (tag, g * PER_HALF))
            nc.tensor.matmul_mx(
                out=bank[:],
                lhsT=w23_codes[:, i * N : (i + 1) * N].bitcast(FP8X4),
                lhsT_scale=w23_scale[:, i * N : (i + 1) * N],
                rhs=codes[:].bitcast(FP8X4),
                rhs_scale=scale[:],
                start=True,
                stop=True,
            )
            return bank

        def make_fd_sq(g):
            fd = second_product(0, "x_bank", zone_bf, g)
            fd_sq[g] = sb("fd_sq%d" % g, HALF, F32)
            nc.scalar.activation(fd_sq[g][:], fd[:], ACT.Square)

        def make_curve(g):
            curve[g] = second_product(1, "e_bank", ztwo_bf, g)

        def weigh(g):
            weighted[g] = sb("weighted%d" % g, HALF, F32)
            nc.vector.tensor_tensor(weighted[g][:], fd_sq[g][:], half_sb[:, g * HALF : (g + 1) * HALF], ALU.mult)

        def finish(g):
            result = sb("result%d" % g, HALF, F32)
            nc.vector.tensor_tensor(result[:], weighted[g][:], curve[g][:], ALU.subtract)
            nc.sync.dma_start(out=out[:, g * HALF : (g + 1) * HALF], in_=result[:])

        for c in range(PER_HALF + 1):
            make_hid(c)
        make_hid_sq(0)
        make_hid(CHUNKS - 1)
        make_slope(0)
        make_hid_sq(1)
        make_slope(1)

        for i in range(2):
            nc.gpsimd.tensor_scalar(
                w23_bf[:, i * PACK * N : (i + 1) * PACK * N].rearrange("p (n j) -> p n j", j=PACK),
                w23_raw[i][:].rearrange("p j n -> p n j"),
                1.0,
                0.0,
                ALU.mult,
                ALU.add,
            )

        for c in range(CHUNKS):
            make_hid_tan(c)
        for c in range(PER_HALF):
            make_zone(c)
        nc.vector.quantize_mx(out=w23_codes[:].bitcast(FP8X4), scales=w23_scale[:], in_=w23_bf[:])
        for c in range(PER_HALF):
            make_ztwo(c)
        for c in range(PER_HALF, CHUNKS):
            make_zone(c)
        for c in range(CHUNKS):
            round_zone(c)

        make_fd_sq(0)
        make_curve(0)
        make_ztwo(CHUNKS - 2)
        make_fd_sq(1)
        make_ztwo(CHUNKS - 1)
        weigh(0)
        make_curve(1)
        weigh(1)
        for g in range(HALVES):
            finish(g)
